import numpy as np, ml_dtypes
CORES = [30,158,46,174,86,214]
N = 6
TK = 512
def setup_inputs(rng):
    return {"c": rng.standard_normal((N, 128, 128), dtype=np.float32).astype(ml_dtypes.bfloat16), "x": rng.standard_normal((N, 128, TK), dtype=np.float32).astype(ml_dtypes.bfloat16)}
def setup_inputs_big(rng):
    d = setup_inputs(rng)
    for k in ("c", "x"): d[k] = (d[k].astype(np.float32) * 1024.0).astype(d[k].dtype)
    return d
def setup_inputs_small(rng):
    d = setup_inputs(rng)
    for k in ("c", "x"): d[k] = (d[k].astype(np.float32) * (1 / 1024.0)).astype(d[k].dtype)
    return d
def setup_inputs_apart(rng):
    d = setup_inputs(rng)
    f = (10.0 ** rng.permutation(np.linspace(-1.5, 1.5, N))).astype(np.float32).reshape(N, 1, 1)
    for k in ("c", "x"): d[k] = (d[k].astype(np.float32) * f).astype(d[k].dtype)
    return d
def reference(c, x):
    C, X = c.astype(np.float64), x.astype(np.float64)
    y = np.zeros((N, 128, TK))
    for r in range(N):
        for j in range(N):
            y[r] += C[(r - j) % N].T @ X[j]
    return {"y": y.astype(ml_dtypes.bfloat16 if x.dtype != np.float64 else np.float64)}

@@ -1,0 +1,80 @@
+from concourse.bass import DstId, RemoteDMATransfer
+
+N = 6
+KC = 128
+TK = 512
+W = KC + TK
+H = TK // 2
+
+SCRATCH = {
+    "land": ("sbuf", [128, N * W], "bfloat16"),
+    "yout": ("sbuf", [128, TK], "bfloat16"),
+    "ps0": ("psum", [128, 512], "float32"),
+    "ps1": ("psum", [128, 512], "float32"),
+}
+SEMAPHORES = ["ld", "sent", "mm0", "mm1", "cp0", "cp1", "st"] + ["arr%d" % j for j in range(N)]
+
+
+def _bits(mask):
+    return bin(mask).count("1")
+
+
+def rank_program(g, core, T, topo):
+    r = T.rank_of(core)
+    if r is None:
+        return
+    sem = T.sem
+
+    def slot(j):
+        return T.land[:, j * W:(j + 1) * W]
+
+    def cmat(k):
+        return T.land[:, k * W:k * W + KC]
+
+    def xhalf(j, h):
+        return T.land[:, j * W + KC + h * H:j * W + KC + (h + 1) * H]
+
+    g.sync.dma_start(cmat(r), T.c[:]).then_inc(sem.ld, 16)
+    g.scalar.dma_start(T.land[:, r * W + KC:(r + 1) * W], T.x[:]).then_inc(sem.ld, 16)
+
+    dsts = [T.cores[(r + m) % N] for m in range(1, N)]
+    mask = topo.mask(core, dsts[0])
+    for d in dsts:
+        mask &= topo.mask(core, d)
+    ne = _bits(mask)
+    ids = []
+    for d in dsts:
+        rid, pid = topo.addr(d, core)
+        ids.append(DstId(rid=rid, pnc=pid))
+    g.wait_ge(sem.ld, 32)
+    g.remote_dma_fused(
+        [RemoteDMATransfer(dst_ids=ids, dma_engine_mask=mask, remote_sem=sem["arr%d" % r],
+                           srcs=[slot(r)], dsts=[slot(r) for _ in dsts], alu_op=0)],
+        local_sem=sem.sent)
+
+    stages = [[] for _ in range(N)]
+    for a in range(N):
+        b = (r - a) % N
+        stages[max(a, b)].append(((r - a) % N, (r - b) % N))
+    ps = [T.ps0, T.ps1]
+    mm = [sem.mm0, sem.mm1]
+    done = [0, 0]
+    g.tensor.wait_ge(sem.ld, 32)
+    for a in range(N):
+        if a > 0:
+            g.tensor.wait_ge(sem["arr%d" % ((r - a) % N)], ne)
+        for h in range(2):
+            for (k, j) in stages[a]:
+                g.tensor.matmul(ps[h][:, 0:H], cmat(k), xhalf(j, h), done[h] == 0, done[h] == N - 1).then_inc(mm[h], 1)
+                done[h] += 1
+
+    g.vector.wait_ge(sem.mm0, N)
+    g.vector.tensor_copy(T.yout[:, 0:H], T.ps0[:, 0:H]).then_inc(sem.cp0, 1)
+    g.vector.wait_ge(sem.mm1, N)
+    g.vector.tensor_copy(T.yout[:, H:TK], T.ps1[:, 0:H]).then_inc(sem.cp1, 1)
+    g.sync.wait_ge(sem.cp0, 1)
+    g.sync.dma_start(T.y[:, 0:H], T.yout[:, 0:H]).then_inc(sem.st, 16)
+    g.scalar.wait_ge(sem.cp1, 1)
+    g.scalar.dma_start(T.y[:, H:TK], T.yout[:, H:TK]).then_inc(sem.st, 16)
+    g.wait_ge(sem.sent, ne)
+    g.wait_ge(sem.st, 32)

@@ -5,6 +5,8 @@ KC = 128
 TK = 512
 W = KC + TK
 H = TK // 2
+NSIM = 256
+NDIRECT = 3
 
 SCRATCH = {
     "land": ("sbuf", [128, N * W], "bfloat16"),
@@ -12,21 +14,60 @@ SCRATCH = {
     "ps0": ("psum", [128, 512], "float32"),
     "ps1": ("psum", [128, 512], "float32"),
 }
-SEMAPHORES = ["ld", "sent", "mm0", "mm1", "cp0", "cp1", "st"] + ["arr%d" % j for j in range(N)]
+SEMAPHORES = ["ld", "sent", "harr", "mm0", "mm1", "cp0", "cp1", "st"] + ["arr%d" % j for j in range(N)]
 
 
 def _bits(mask):
     return bin(mask).count("1")
 
 
+def _plan(q, T, topo):
+    rc = T.cores[q]
+    direct = [T.cores[(q + m) % N] for m in range(1, NDIRECT + 1)]
+    fwd = [T.cores[(q + m) % N] for m in range(NDIRECT + 1, N)]
+    for h in range(NSIM):
+        if T.rank_of(h) is not None or topo.host(h) != topo.host(rc) or topo.chip(h) != topo.chip(rc):
+            continue
+        if topo.die(h) != topo.die(rc) and all(topo.may_write(h, d) for d in fwd):
+            return rc, direct, h, fwd
+    return rc, direct, None, fwd
+
+
+def _common_mask(src, dsts, topo):
+    m = topo.mask(src, dsts[0])
+    for d in dsts:
+        m &= topo.mask(src, d)
+    return m
+
+
+def _send(g, src, dsts, mask, ap, remote_sem, local_sem, topo):
+    ids = []
+    for d in dsts:
+        rid, pid = topo.addr(d, src)
+        ids.append(DstId(rid=rid, pnc=pid))
+    g.remote_dma_fused(
+        [RemoteDMATransfer(dst_ids=ids, dma_engine_mask=mask, remote_sem=remote_sem,
+                           srcs=[ap], dsts=[ap for _ in dsts], alu_op=0)],
+        local_sem=local_sem)
+
+
 def rank_program(g, core, T, topo):
-    r = T.rank_of(core)
-    if r is None:
-        return
     sem = T.sem
 
     def slot(j):
         return T.land[:, j * W:(j + 1) * W]
+
+    r = T.rank_of(core)
+    if r is None:
+        for q in range(N):
+            rc, direct, hc, fwd = _plan(q, T, topo)
+            if hc == core:
+                onm = topo.mask(rc, hc) & ~_common_mask(rc, direct, topo)
+                m = _common_mask(hc, fwd, topo)
+                g.wait_ge(sem.harr, _bits(onm))
+                _send(g, hc, fwd, m, slot(q), sem["arr%d" % q], sem.sent, topo)
+                g.wait_ge(sem.sent, _bits(m))
+        return
 
     def cmat(k):
         return T.land[:, k * W:k * W + KC]
@@ -37,20 +78,13 @@ def rank_program(g, core, T, topo):
     g.sync.dma_start(cmat(r), T.c[:]).then_inc(sem.ld, 16)
     g.scalar.dma_start(T.land[:, r * W + KC:(r + 1) * W], T.x[:]).then_inc(sem.ld, 16)
 
-    dsts = [T.cores[(r + m) % N] for m in range(1, N)]
-    mask = topo.mask(core, dsts[0])
-    for d in dsts:
-        mask &= topo.mask(core, d)
-    ne = _bits(mask)
-    ids = []
-    for d in dsts:
-        rid, pid = topo.addr(d, core)
-        ids.append(DstId(rid=rid, pnc=pid))
+    rc, direct, hc, fwd = _plan(r, T, topo)
+    offm = _common_mask(core, direct, topo)
+    onm = topo.mask(core, hc) & ~offm
+    ne = _bits(offm)
     g.wait_ge(sem.ld, 32)
-    g.remote_dma_fused(
-        [RemoteDMATransfer(dst_ids=ids, dma_engine_mask=mask, remote_sem=sem["arr%d" % r],
-                           srcs=[slot(r)], dsts=[slot(r) for _ in dsts], alu_op=0)],
-        local_sem=sem.sent)
+    _send(g, core, [hc], onm, slot(r), sem.harr, sem.sent, topo)
+    _send(g, core, direct, offm, slot(r), sem["arr%d" % r], sem.sent, topo)
 
     stages = [[] for _ in range(N)]
     for a in range(N):
@@ -76,5 +110,5 @@ def rank_program(g, core, T, topo):
     g.sync.dma_start(T.y[:, 0:H], T.yout[:, 0:H]).then_inc(sem.st, 16)
     g.scalar.wait_ge(sem.cp1, 1)
     g.scalar.dma_start(T.y[:, H:TK], T.yout[:, H:TK]).then_inc(sem.st, 16)
-    g.wait_ge(sem.sent, ne)
+    g.wait_ge(sem.sent, ne + _bits(onm))
     g.wait_ge(sem.st, 32)

@@ -6,7 +6,7 @@ TK = 512
 W = KC + TK
 H = TK // 2
 NSIM = 256
-NDIRECT = 3
+NNEAR = 3
 
 SCRATCH = {
     "land": ("sbuf", [128, N * W], "bfloat16"),
@@ -14,7 +14,9 @@ SCRATCH = {
     "ps0": ("psum", [128, 512], "float32"),
     "ps1": ("psum", [128, 512], "float32"),
 }
-SEMAPHORES = ["ld", "sent", "harr", "mm0", "mm1", "cp0", "cp1", "st"] + ["arr%d" % j for j in range(N)]
+SEMAPHORES = (["ldl", "ldh", "ldc", "sent", "hc", "hlo", "hhi", "mm0", "mm1", "cp0", "cp1", "st"]
+              + ["cs%d" % j for j in range(N)] + ["arr%d" % j for j in range(N)]
+              + ["xl%d" % j for j in range(N)] + ["xh%d" % j for j in range(N)])
 
 
 def _bits(mask):
@@ -23,14 +25,14 @@ def _bits(mask):
 
 def _plan(q, T, topo):
     rc = T.cores[q]
-    direct = [T.cores[(q + m) % N] for m in range(1, NDIRECT + 1)]
-    fwd = [T.cores[(q + m) % N] for m in range(NDIRECT + 1, N)]
+    near = [T.cores[(q + m) % N] for m in range(1, NNEAR + 1)]
+    far = [T.cores[(q + m) % N] for m in range(NNEAR + 1, N)]
     for h in range(NSIM):
         if T.rank_of(h) is not None or topo.host(h) != topo.host(rc) or topo.chip(h) != topo.chip(rc):
             continue
-        if topo.die(h) != topo.die(rc) and all(topo.may_write(h, d) for d in fwd):
-            return rc, direct, h, fwd
-    return rc, direct, None, fwd
+        if topo.die(h) != topo.die(rc) and all(topo.may_write(h, d) for d in far):
+            return rc, near, far, h
+    return rc, near, far, None
 
 
 def _common_mask(src, dsts, topo):
@@ -40,34 +42,17 @@ def _common_mask(src, dsts, topo):
     return m
 
 
-def _send(g, src, dsts, mask, ap, remote_sem, local_sem, topo):
+def _tr(src, dsts, mask, ap, remote_sem, topo):
     ids = []
     for d in dsts:
         rid, pid = topo.addr(d, src)
         ids.append(DstId(rid=rid, pnc=pid))
-    g.remote_dma_fused(
-        [RemoteDMATransfer(dst_ids=ids, dma_engine_mask=mask, remote_sem=remote_sem,
-                           srcs=[ap], dsts=[ap for _ in dsts], alu_op=0)],
-        local_sem=local_sem)
+    return RemoteDMATransfer(dst_ids=ids, dma_engine_mask=mask, remote_sem=remote_sem,
+                             srcs=[ap], dsts=[ap for _ in dsts], alu_op=0)
 
 
 def rank_program(g, core, T, topo):
     sem = T.sem
-
-    def slot(j):
-        return T.land[:, j * W:(j + 1) * W]
-
-    r = T.rank_of(core)
-    if r is None:
-        for q in range(N):
-            rc, direct, hc, fwd = _plan(q, T, topo)
-            if hc == core:
-                onm = topo.mask(rc, hc) & ~_common_mask(rc, direct, topo)
-                m = _common_mask(hc, fwd, topo)
-                g.wait_ge(sem.harr, _bits(onm))
-                _send(g, hc, fwd, m, slot(q), sem["arr%d" % q], sem.sent, topo)
-                g.wait_ge(sem.sent, _bits(m))
-        return
 
     def cmat(k):
         return T.land[:, k * W:k * W + KC]
@@ -75,32 +60,82 @@ def rank_program(g, core, T, topo):
     def xhalf(j, h):
         return T.land[:, j * W + KC + h * H:j * W + KC + (h + 1) * H]
 
-    g.sync.dma_start(cmat(r), T.c[:]).then_inc(sem.ld, 16)
-    g.scalar.dma_start(T.land[:, r * W + KC:(r + 1) * W], T.x[:]).then_inc(sem.ld, 16)
+    def xall(j):
+        return T.land[:, j * W + KC:(j + 1) * W]
 
-    rc, direct, hc, fwd = _plan(r, T, topo)
-    offm = _common_mask(core, direct, topo)
+    r = T.rank_of(core)
+    if r is None:
+        for q in range(N):
+            rc, near, far, hc = _plan(q, T, topo)
+            if hc == core:
+                non = _bits(topo.mask(rc, hc) & ~_common_mask(rc, near, topo))
+                m = _common_mask(hc, far, topo)
+                g.wait_ge(sem.hc, non)
+                g.remote_dma_fused([_tr(hc, far, m, cmat(q), sem["cs%d" % q], topo)], local_sem=sem.sent)
+                g.wait_ge(sem.hlo, non)
+                g.remote_dma_fused([_tr(hc, far, m, xhalf(q, 0), sem["xl%d" % q], topo)], local_sem=sem.sent)
+                g.wait_ge(sem.hhi, non)
+                g.remote_dma_fused([_tr(hc, far, m, xhalf(q, 1), sem["xh%d" % q], topo)], local_sem=sem.sent)
+                g.wait_ge(sem.sent, 3 * _bits(m))
+        return
+
+    g.scalar.dma_start(cmat(r), T.c[:]).then_inc(sem.ldc, 16)
+    g.sync.dma_start(xhalf(r, 0), T.x[:, 0:H]).then_inc(sem.ldl, 16)
+    g.scalar.dma_start(xhalf(r, 1), T.x[:, H:TK]).then_inc(sem.ldh, 16)
+
+    rc, near, far, hc = _plan(r, T, topo)
+    offm = _common_mask(core, near, topo)
     onm = topo.mask(core, hc) & ~offm
     ne = _bits(offm)
-    g.wait_ge(sem.ld, 32)
-    _send(g, core, [hc], onm, slot(r), sem.harr, sem.sent, topo)
-    _send(g, core, direct, offm, slot(r), sem["arr%d" % r], sem.sent, topo)
+    g.wait_ge(sem.ldc, 16)
+    g.remote_dma_fused([_tr(core, [hc], onm, cmat(r), sem.hc, topo),
+                        _tr(core, near, offm, cmat(r), sem["cs%d" % r], topo)], local_sem=sem.sent)
+    g.wait_ge(sem.ldl, 16)
+    g.remote_dma_fused([_tr(core, [hc], onm, xhalf(r, 0), sem.hlo, topo)], local_sem=sem.sent)
+    g.wait_ge(sem.ldh, 16)
+    g.remote_dma_fused([_tr(core, near, offm, xall(r), sem["arr%d" % r], topo)], local_sem=sem.sent)
+    g.remote_dma_fused([_tr(core, [hc], onm, xhalf(r, 1), sem.hhi, topo)], local_sem=sem.sent)
 
-    stages = [[] for _ in range(N)]
+    def t_c(a):
+        if a <= NNEAR:
+            return 0.2 * a
+        return 1.0 + 0.2 * (a - NNEAR)
+
+    def t_x(a, h):
+        if a == 0:
+            return 0.0
+        if a <= NNEAR:
+            return 0.2 * NNEAR + 0.8 * a
+        return 1.45 + 0.4 * (a - NNEAR + (N - 1 - NNEAR) * h)
+
+    items = []
     for a in range(N):
         b = (r - a) % N
-        stages[max(a, b)].append(((r - a) % N, (r - b) % N))
+        for h in range(2):
+            items.append((max(t_c(a), t_x(b, h)), h, a, b))
+    items.sort()
     ps = [T.ps0, T.ps1]
     mm = [sem.mm0, sem.mm1]
     done = [0, 0]
-    g.tensor.wait_ge(sem.ld, 32)
-    for a in range(N):
+    waited = []
+    g.tensor.wait_ge(sem.ldc, 16)
+    g.tensor.wait_ge(sem.ldl, 16)
+    g.tensor.wait_ge(sem.ldh, 16)
+    for (_, h, a, b) in items:
+        k, j = (r - a) % N, (r - b) % N
+        need = []
         if a > 0:
-            g.tensor.wait_ge(sem["arr%d" % ((r - a) % N)], ne)
-        for h in range(2):
-            for (k, j) in stages[a]:
-                g.tensor.matmul(ps[h][:, 0:H], cmat(k), xhalf(j, h), done[h] == 0, done[h] == N - 1).then_inc(mm[h], 1)
-                done[h] += 1
+            need.append("cs%d" % k)
+        if 0 < b <= NNEAR:
+            need.append("arr%d" % j)
+        elif b > NNEAR:
+            need.append(("xl%d" if h == 0 else "xh%d") % j)
+        for s in need:
+            if s not in waited:
+                g.tensor.wait_ge(sem[s], ne)
+                waited.append(s)
+        g.tensor.matmul(ps[h][:, 0:H], cmat(k), xhalf(j, h), done[h] == 0, done[h] == N - 1).then_inc(mm[h], 1)
+        done[h] += 1
 
     g.vector.wait_ge(sem.mm0, N)
     g.vector.tensor_copy(T.yout[:, 0:H], T.ps0[:, 0:H]).then_inc(sem.cp0, 1)
@@ -110,5 +145,5 @@ def rank_program(g, core, T, topo):
     g.sync.dma_start(T.y[:, 0:H], T.yout[:, 0:H]).then_inc(sem.st, 16)
     g.scalar.wait_ge(sem.cp1, 1)
     g.scalar.dma_start(T.y[:, H:TK], T.yout[:, H:TK]).then_inc(sem.st, 16)
-    g.wait_ge(sem.sent, ne + _bits(onm))
+    g.wait_ge(sem.sent, 2 * ne + 3 * _bits(onm))
     g.wait_ge(sem.st, 32)

from concourse.bass import DstId, RemoteDMATransfer

N = 6
KC = 128
TK = 512
W = KC + TK
H = TK // 2
NSIM = 256
NNEAR = 3

SCRATCH = {
    "land": ("sbuf", [128, N * W], "bfloat16"),
    "yout": ("sbuf", [128, TK], "bfloat16"),
    "ps0": ("psum", [128, 512], "float32"),
    "ps1": ("psum", [128, 512], "float32"),
}
SEMAPHORES = (["ldl", "ldh", "ldc", "sent", "hc", "hlo", "hhi", "mm0", "mm1", "cp0", "cp1", "st"]
              + ["cs%d" % j for j in range(N)] + ["arr%d" % j for j in range(N)]
              + ["xl%d" % j for j in range(N)] + ["xh%d" % j for j in range(N)])


def _bits(mask):
    return bin(mask).count("1")


def _plan(q, T, topo):
    rc = T.cores[q]
    near = [T.cores[(q + m) % N] for m in range(1, NNEAR + 1)]
    far = [T.cores[(q + m) % N] for m in range(NNEAR + 1, N)]
    for h in range(NSIM):
        if T.rank_of(h) is not None or topo.host(h) != topo.host(rc) or topo.chip(h) != topo.chip(rc):
            continue
        if topo.die(h) != topo.die(rc) and all(topo.may_write(h, d) for d in far):
            return rc, near, far, h
    return rc, near, far, None


def _common_mask(src, dsts, topo):
    m = topo.mask(src, dsts[0])
    for d in dsts:
        m &= topo.mask(src, d)
    return m


def _tr(src, dsts, mask, ap, remote_sem, topo):
    ids = []
    for d in dsts:
        rid, pid = topo.addr(d, src)
        ids.append(DstId(rid=rid, pnc=pid))
    return RemoteDMATransfer(dst_ids=ids, dma_engine_mask=mask, remote_sem=remote_sem,
                             srcs=[ap], dsts=[ap for _ in dsts], alu_op=0)


def rank_program(g, core, T, topo):
    sem = T.sem

    def cmat(k):
        return T.land[:, k * W:k * W + KC]

    def xhalf(j, h):
        return T.land[:, j * W + KC + h * H:j * W + KC + (h + 1) * H]

    def xall(j):
        return T.land[:, j * W + KC:(j + 1) * W]

    r = T.rank_of(core)
    if r is None:
        for q in range(N):
            rc, near, far, hc = _plan(q, T, topo)
            if hc == core:
                non = _bits(topo.mask(rc, hc) & ~_common_mask(rc, near, topo))
                m = _common_mask(hc, far, topo)
                g.wait_ge(sem.hc, non)
                g.remote_dma_fused([_tr(hc, far, m, cmat(q), sem["cs%d" % q], topo)], local_sem=sem.sent)
                g.wait_ge(sem.hlo, non)
                g.remote_dma_fused([_tr(hc, far, m, xhalf(q, 0), sem["xl%d" % q], topo)], local_sem=sem.sent)
                g.wait_ge(sem.hhi, non)
                g.remote_dma_fused([_tr(hc, far, m, xhalf(q, 1), sem["xh%d" % q], topo)], local_sem=sem.sent)
                g.wait_ge(sem.sent, 3 * _bits(m))
        return

    g.scalar.dma_start(cmat(r), T.c[:]).then_inc(sem.ldc, 16)
    g.sync.dma_start(xhalf(r, 0), T.x[:, 0:H]).then_inc(sem.ldl, 16)
    g.scalar.dma_start(xhalf(r, 1), T.x[:, H:TK]).then_inc(sem.ldh, 16)

    rc, near, far, hc = _plan(r, T, topo)
    offm = _common_mask(core, near, topo)
    onm = topo.mask(core, hc) & ~offm
    ne = _bits(offm)
    g.wait_ge(sem.ldc, 16)
    g.remote_dma_fused([_tr(core, [hc], onm, cmat(r), sem.hc, topo),
                        _tr(core, near, offm, cmat(r), sem["cs%d" % r], topo)], local_sem=sem.sent)
    g.wait_ge(sem.ldl, 16)
    g.remote_dma_fused([_tr(core, [hc], onm, xhalf(r, 0), sem.hlo, topo)], local_sem=sem.sent)
    g.wait_ge(sem.ldh, 16)
    g.remote_dma_fused([_tr(core, near, offm, xall(r), sem["arr%d" % r], topo)], local_sem=sem.sent)
    g.remote_dma_fused([_tr(core, [hc], onm, xhalf(r, 1), sem.hhi, topo)], local_sem=sem.sent)

    def t_c(a):
        if a <= NNEAR:
            return 0.2 * a
        return 1.0 + 0.2 * (a - NNEAR)

    def t_x(a, h):
        if a == 0:
            return 0.0
        if a <= NNEAR:
            return 0.2 * NNEAR + 0.8 * a
        return 1.45 + 0.4 * (a - NNEAR + (N - 1 - NNEAR) * h)

    items = []
    for a in range(N):
        b = (r - a) % N
        for h in range(2):
            items.append((max(t_c(a), t_x(b, h)), h, a, b))
    items.sort()
    ps = [T.ps0, T.ps1]
    mm = [sem.mm0, sem.mm1]
    done = [0, 0]
    waited = []
    g.tensor.wait_ge(sem.ldc, 16)
    g.tensor.wait_ge(sem.ldl, 16)
    g.tensor.wait_ge(sem.ldh, 16)
    for (_, h, a, b) in items:
        k, j = (r - a) % N, (r - b) % N
        need = []
        if a > 0:
            need.append("cs%d" % k)
        if 0 < b <= NNEAR:
            need.append("arr%d" % j)
        elif b > NNEAR:
            need.append(("xl%d" if h == 0 else "xh%d") % j)
        for s in need:
            if s not in waited:
                g.tensor.wait_ge(sem[s], ne)
                waited.append(s)
        g.tensor.matmul(ps[h][:, 0:H], cmat(k), xhalf(j, h), done[h] == 0, done[h] == N - 1).then_inc(mm[h], 1)
        done[h] += 1

    g.vector.wait_ge(sem.mm0, N)
    g.vector.tensor_copy(T.yout[:, 0:H], T.ps0[:, 0:H]).then_inc(sem.cp0, 1)
    g.vector.wait_ge(sem.mm1, N)
    g.vector.tensor_copy(T.yout[:, H:TK], T.ps1[:, 0:H]).then_inc(sem.cp1, 1)
    g.sync.wait_ge(sem.cp0, 1)
    g.sync.dma_start(T.y[:, 0:H], T.yout[:, 0:H]).then_inc(sem.st, 16)
    g.scalar.wait_ge(sem.cp1, 1)
    g.scalar.dma_start(T.y[:, H:TK], T.yout[:, H:TK]).then_inc(sem.st, 16)
    g.wait_ge(sem.sent, 2 * ne + 3 * _bits(onm))
    g.wait_ge(sem.st, 32)
